import numpy as np
import ml_dtypes


def mxq(x, axis, fmt="e4m3"):
    dtype, down = {"e4m3": (ml_dtypes.float8_e4m3fn, 7), "e5m2": (ml_dtypes.float8_e5m2, 14)}[fmt]
    v = np.moveaxis(np.asarray(x, np.float32).astype(ml_dtypes.bfloat16).astype(np.float64), axis, -1)
    blocks = v.reshape(v.shape[:-1] + (-1, 32))
    amax = np.abs(blocks).max(-1, keepdims=True)
    byte = np.maximum(np.where(amax > 0, np.frexp(amax)[1] - 1 + 127, 0) - down, 1)
    scale = np.exp2(byte - 127.0)
    codes = (blocks / scale).astype(np.float32).astype(dtype).astype(np.float64)
    return np.moveaxis((codes * scale).reshape(v.shape), -1, axis)


WIDE = False


def mx_kscale(k):
    if not WIDE:
        return np.ones(k)
    levels = np.array([10, -10, 5, -5, 0])
    if k % 512:
        return np.exp2(np.random.permutation(np.resize(levels, k // 32))).repeat(32)
    a = np.empty((k // 512, 16))
    for p in range(k // 512):
        a[p, :8] = np.random.permutation(np.resize(levels, 8))
        for g in range(8):
            far = levels[np.abs(levels - a[p, g]) >= 10]
            a[p, g + 8] = far[np.random.randint(len(far))]
    return np.exp2(a.ravel()).repeat(32)


def f64(x):
    return np.asarray(x).astype(np.float64)


def striped(idx):
    return np.tile(idx.reshape(-1, 16).T, (8, 1)).astype(np.uint16)


def unstriped(offs):
    return offs[:16].T.reshape(-1).astype(np.int64)


E2M1 = np.array([0.0, 0.5, 1.0, 1.5, 2.0, 3.0, 4.0, 6.0, -0.0, -0.5, -1.0, -1.5, -2.0, -3.0, -4.0, -6.0])


def pack_weight(w, fmt):
    k, n = w.shape
    w = f64(np.asarray(w, np.float32).astype(ml_dtypes.bfloat16)).reshape(k // 32, 32, n)
    amax = np.abs(w).max(1)
    if fmt == "e4m3":
        byte = np.frexp(amax)[1] - 1 + 127 - 7
    else:
        mant, ex = np.frexp(amax / 6.0)
        byte = np.where(mant > 0.5, ex, ex - 1) + 127
    byte = np.clip(np.where(amax > 0, byte, 1), 1, 254)
    scaled = (w * np.exp2(127.0 - byte)[:, None, :]).reshape(k, n).astype(np.float32)
    by_word = np.ascontiguousarray(scaled.reshape(k // 512, 128, 4, n).transpose(0, 1, 3, 2))
    if fmt == "e4m3":
        words = by_word.astype(ml_dtypes.float8_e4m3fn).view(np.uint8)
    else:
        c = by_word.astype(ml_dtypes.float4_e2m1fn).view(np.uint8) & 0xF
        words = (c[..., 0::2] | (c[..., 1::2] << 4)).reshape(k // 512, 128, 2 * n)
    return np.ascontiguousarray(words), np.ascontiguousarray(byte.astype(np.uint8).reshape(k // 512, 16, n))


def unpack_weight(words, scales, fmt):
    g, _, n = scales.shape
    words = np.ascontiguousarray(words).reshape(g, 128, n, -1)
    if fmt == "e4m3":
        vals = words.view(ml_dtypes.float8_e4m3fn).astype(np.float64)
    else:
        nib = np.empty((g, 128, n, 4), np.uint8)
        nib[..., 0::2] = words & 0xF
        nib[..., 1::2] = words >> 4
        vals = E2M1[nib]
    vals = vals * np.repeat(np.exp2(scales.astype(np.float64) - 127.0), 8, axis=1)[..., None]
    return vals.transpose(0, 1, 3, 2).reshape(g * 512, n)


def gelu(v):
    return 0.5 * v * (1.0 + np.tanh(np.sqrt(2.0 / np.pi) * (v + 0.044715 * v**3)))


def bf(x):
    return np.asarray(x, np.float32).astype(ml_dtypes.bfloat16)

def planes(Y):
    n, m = Y.shape
    b = f64(bf(Y)).reshape(n // 32, 32, m)
    amax = np.abs(b).max(1)
    byte = np.clip(np.where(amax > 0, np.frexp(amax)[1] - 1 + 127 - 7, 1), 1, 254)
    codes = (b * np.exp2(127.0 - byte)[:, None, :]).reshape(n, m).astype(np.float32).astype(ml_dtypes.float8_e4m3fn).view(np.uint8)
    words = codes.reshape(n // 512, 128, 4, m).transpose(0, 1, 3, 2)
    return np.ascontiguousarray(words), np.ascontiguousarray(byte.astype(np.uint8).reshape(n // 512, 16, m))


K, H, N, T, S = 512, 1024, 512, 4096, 1024

def setup_inputs():
    n = np.random.standard_normal
    s = mx_kscale(K)[:, None]
    u = mx_kscale(H)[:, None]
    gain = np.exp(0.8 * n(N))
    tab_words, tab_scales = pack_weight(n((K, T)) * s, "e4m3")
    wa_words, wa_scales = pack_weight(n((K, H)) / np.sqrt(K) / s * u.T, "e2m1")
    wb_words, wb_scales = pack_weight(n((K, H)) / np.sqrt(K) / s * u.T, "e4m3")
    return {
        "tab_words": tab_words, "tab_scales": tab_scales,
        "offs": striped(np.random.permutation(T)[:S]),
        "wq": (n((K, H)) / np.sqrt(K) / s).astype(np.float32),
        "wa_words": wa_words, "wa_scales": wa_scales,
        "wb_words": wb_words, "wb_scales": wb_scales,
        "ws": (n((H, N)) / np.sqrt(H) / u * gain).astype(np.float32),
        "base": (0.5 * n(N) * gain).astype(np.float32),
    }

def reference(tab_words, tab_scales, offs, wq, wa_words, wa_scales, wb_words, wb_scales, ws, base):
    v = unpack_weight(tab_words, tab_scales, "e4m3")[:, unstriped(offs)]
    wa = unpack_weight(wa_words, wa_scales, "e2m1")
    wb = unpack_weight(wb_words, wb_scales, "e4m3")
    route = mxq(f64(wq), 0, "e4m3").T @ v
    left = wa.T @ v
    right = wb.T @ v
    h = np.abs(route) * np.where(route > 0, left, right)
    y = (mxq(f64(ws), 0, "e4m3").T @ mxq(h, 0, "e4m3")) + f64(base)[:, None]
    words, scales = planes(y)
    return y, words, scales

@@ -1,0 +1,295 @@
+from contextlib import ExitStack
+
+import concourse.mybir as mybir
+
+K, H, N, T, S = 512, 1024, 512, 4096, 1024
+FLOPS = 2 * S * (3 * K * H + H * N)
+
+F32 = mybir.dt.float32
+BF16 = mybir.dt.bfloat16
+I32 = mybir.dt.int32
+U32 = mybir.dt.uint32
+U16 = mybir.dt.uint16
+U8 = mybir.dt.uint8
+FP8X4 = mybir.dt.float8_e4m3fn_x4
+FP4X4 = mybir.dt.float4_e2m1fn_x4
+ALU = mybir.AluOpType
+ACT = mybir.ActivationFunctionType
+
+P = 128
+PACK = 4
+PASS = P * PACK
+RUN = 8
+BLOCKS = PASS // (RUN * PACK)
+CHUNK = 128
+QUADS = 4
+WB_ROW = 4
+
+
+def tile_list_routed_credit_scorecard_kernel(
+    tc, tab_words, tab_scales, offs, wq, wa_words, wa_scales, wb_words, wb_scales, ws, base, out_0, out_1, out_2
+):
+    nc = tc.nc
+    with ExitStack() as ctx:
+        keep = ctx.enter_context(tc.tile_pool(name="keep", bufs=1))
+        wq_stage = ctx.enter_context(tc.tile_pool(name="wq_stage", bufs=1))
+        ring = ctx.enter_context(tc.tile_pool(name="ring", bufs=2))
+        work = ctx.enter_context(tc.tile_pool(name="work", bufs=2))
+        psum = ctx.enter_context(tc.psum_pool(name="psum", bufs=2))
+
+        offsets = keep.tile([P, S // 16], U16, name="offsets")
+        tab_w = keep.tile([P, T], U32, name="tab_w", align_bytes=64)
+        tab_s = keep.tile([P, T], U8, name="tab_s", align_bytes=64)
+        v_w = keep.tile([P, S], U32, name="v_w", align_bytes=64)
+        v_s = keep.tile([P, S], U8, name="v_s", align_bytes=64)
+        wab_s_raw = keep.tile([P, H], U8, name="wab_s_raw", align_bytes=64)
+        wab_s = keep.tile([P, H], U8, name="wab_s", align_bytes=64)
+        base_sb = keep.tile([P, PACK], F32, name="base_sb")
+        wq_w = [keep.tile([P, PASS], U32, name="wq_w%d" % b, align_bytes=64) for b in range(2)]
+        wq_s = [keep.tile([P, PASS], U8, name="wq_s%d" % b, align_bytes=64) for b in range(2)]
+        wa_w = [keep.tile([P, 2 * PASS], U8, name="wa_w%d" % b, align_bytes=64) for b in range(2)]
+        wb_w = [keep.tile([P, PASS], U32, name="wb_w%d" % b, align_bytes=64) for b in range(2)]
+        ws_w = [keep.tile([P, N], U32, name="ws_w%d" % b, align_bytes=64) for b in range(2)]
+        ws_s = [keep.tile([P, N], U8, name="ws_s%d" % b, align_bytes=64) for b in range(2)]
+        h_w = [keep.tile([P, S], U32, name="h_w%d" % b, align_bytes=64) for b in range(2)]
+        h_s = [keep.tile([P, S], U8, name="h_s%d" % b, align_bytes=64) for b in range(2)]
+        y_w = keep.tile([P, S], U32, name="y_w", align_bytes=64)
+        y_s = keep.tile([P, S], U8, name="y_s", align_bytes=64)
+
+        wq_rows = wq.rearrange("(p j) r -> p j r", j=PACK)
+        wa_src = wa_words[0].bitcast(I32)
+        wb_src = wb_words[0].rearrange("p c i -> p (c i)").bitcast(I32)
+        y_rows = out_0.rearrange("(p s) j -> p s j", s=PACK)
+        y_w_dst = out_1[0].rearrange("p m t -> p (m t)").bitcast(I32)
+
+        raw = {}
+        rounded = {}
+
+        def load_wq(b):
+            raw["wq", b] = wq_stage.tile([P, PACK, PASS], F32, name="wq_raw")
+            nc.sync.dma_start(out=raw["wq", b][:], in_=wq_rows[:, :, PASS * b : PASS * (b + 1)])
+
+        def load_wab(b):
+            raw["wa", b] = ring.tile([P, PASS // 2], I32, name="wa_raw", tag="ring")
+            nc.sync.dma_start(out=raw["wa", b][:], in_=wa_src[:, PASS // 2 * b : PASS // 2 * (b + 1)])
+            raw["wb", b] = ring.tile([P, PASS], I32, name="wb_raw", tag="ring")
+            nc.sync.dma_start(out=raw["wb", b][:], in_=wb_src[:, PASS * b : PASS * (b + 1)])
+
+        def load_ws(b):
+            raw["ws", b] = ring.tile([P, PACK, N], F32, name="ws_raw", tag="ring")
+            rows = ws[PASS * b : PASS * (b + 1), :].rearrange("(q t i) n -> t q i n", t=PACK, i=RUN)
+            for t in range(PACK):
+                nc.sync.dma_start(out=raw["ws", b][:, t, :], in_=rows[t])
+
+        def deal_wab(b):
+            nc.vector.tensor_copy(
+                out=wa_w[b][:].bitcast(I32).rearrange("p (t q i) -> p t q i", t=PACK, q=BLOCKS),
+                in_=raw["wa", b][:].rearrange("p (q t i) -> p t q i", t=PACK, q=BLOCKS),
+            )
+            nc.vector.tensor_copy(
+                out=wb_w[b][:].bitcast(I32).rearrange("p (t q i) -> p t q i", t=PACK, q=BLOCKS),
+                in_=raw["wb", b][:].rearrange("p (q t i) -> p t q i", t=PACK, q=BLOCKS),
+            )
+
+        def round_wq(b, t):
+            if t == 0:
+                rounded["wq", b] = work.tile([P, PASS * PACK], BF16, name="w_bf", tag="w_bf", align_bytes=64)
+            dst = rounded["wq", b][:].rearrange("p (t q i j) -> p t q j i", t=PACK, q=BLOCKS, j=PACK)
+            src = raw["wq", b][:].rearrange("p j (q t i) -> p t q j i", t=PACK, i=RUN)
+            nc.scalar.activation(out=dst[:, t], in_=src[:, t], func=ACT.Identity)
+
+        def round_ws(b, part):
+            if part == 0:
+                rounded["ws", b] = work.tile([P, N * PACK], BF16, name="w_bf", tag="w_bf", align_bytes=64)
+            ms = slice(32 * part, 32 * (part + 1))
+            dst = rounded["ws", b][:].rearrange("p (s m t) -> p m t s", s=PACK, t=PACK)
+            src = raw["ws", b][:].rearrange("p t (m s) -> p m t s", s=PACK)
+            nc.scalar.activation(out=dst[:, ms], in_=src[:, ms], func=ACT.Identity)
+
+        def quantize_w(kind, b):
+            words, scales = (wq_w, wq_s) if kind == "wq" else (ws_w, ws_s)
+            nc.vector.quantize_mx(out=words[b][:].bitcast(FP8X4), scales=scales[b][:], in_=rounded[kind, b][:])
+
+        def gather_words(j0, j1):
+            nc.vector.tensor_copy(out=v_w[:, j0:j1], in_=tab_w[:].indirect(offsets[:, j0 // 16 : j1 // 16]))
+
+        banks = {}
+        halves = {}
+        h_bf = {}
+
+        def products(unit):
+            b, c = unit
+            js = slice(CHUNK * c, CHUNK * (c + 1))
+            route = psum.tile([P, PACK, CHUNK], F32, name="route")
+            left = psum.tile([P, PACK, CHUNK], F32, name="left")
+            right = psum.tile([P, PACK, CHUNK], F32, name="right")
+            moving = dict_moving(js)
+            for t in range(PACK):
+                cols = slice(P * t, P * (t + 1))
+                nc.tensor.matmul_mx(out=route[:, t, :], lhsT=wq_w[b][:, cols].bitcast(FP8X4), lhsT_scale=wq_s[b][:, cols],
+                                    rhs=moving[0], rhs_scale=moving[1], start=True, stop=True)
+            route_sb = work.tile([P, CHUNK, PACK], F32, name="route_sb")
+            nc.scalar.copy(out=route_sb[:], in_=route[:].rearrange("p t n -> p n t"))
+            for t in range(PACK):
+                scols = slice(PASS * b + P * t, PASS * b + P * (t + 1))
+                nc.tensor.matmul_mx(out=left[:, t, :], lhsT=wa_w[b][:, 2 * P * t : 2 * P * (t + 1)].bitcast(FP4X4),
+                                    lhsT_scale=wab_s[:, scols], rhs=moving[0], rhs_scale=moving[1], start=True, stop=True)
+            for t in range(PACK):
+                cols = slice(P * t, P * (t + 1))
+                scols = slice(PASS * b + P * t, PASS * b + P * (t + 1))
+                nc.tensor.matmul_mx(out=right[:, t, :], lhsT=wb_w[b][:, cols].bitcast(FP8X4),
+                                    lhsT_scale=wab_s[WB_ROW:P, scols], rhs=moving[0], rhs_scale=moving[1], start=True, stop=True)
+            banks[unit] = (route_sb, left, right)
+
+        def dict_moving(js):
+            return v_w[:, js].bitcast(FP8X4), v_s[:, js]
+
+        def weigh(unit, side):
+            route_sb = banks[unit][0]
+            half = work.tile([P, CHUNK, PACK], BF16, name="half%d" % side, align_bytes=64)
+            nc.vector.scalar_tensor_tensor(
+                out=half[:], in0=route_sb[:], scalar=0.0, in1=banks[unit][1 + side][:].rearrange("p t n -> p n t"),
+                op0=ALU.max if side == 0 else ALU.min, op1=ALU.mult,
+            )
+            halves[unit, side] = half
+
+        def join(unit):
+            h_bf[unit] = work.tile([P, CHUNK * PACK], BF16, name="h_bf", align_bytes=64)
+            nc.vector.tensor_tensor(
+                out=h_bf[unit][:], in0=halves[unit, 0][:].rearrange("p n t -> p (n t)"),
+                in1=halves[unit, 1][:].rearrange("p n t -> p (n t)"), op=ALU.subtract,
+            )
+
+        def quantize_h(unit):
+            b, c = unit
+            js = slice(CHUNK * c, CHUNK * (c + 1))
+            nc.vector.quantize_mx(out=h_w[b][:, js].bitcast(FP8X4), scales=h_s[b][:, js], in_=h_bf[unit][:])
+
+        y_sb = {}
+        y_bf = {}
+
+        def score_pass(bank, s, b, js, start, stop):
+            cols = slice(P * s, P * (s + 1))
+            nc.tensor.matmul_mx(out=bank, lhsT=ws_w[b][:, cols].bitcast(FP8X4), lhsT_scale=ws_s[b][:, cols],
+                                rhs=h_w[b][:, js].bitcast(FP8X4), rhs_scale=h_s[b][:, js], start=start, stop=stop)
+
+        def score(j0, width):
+            js = slice(j0, j0 + width)
+            y_sb[j0] = work.tile([P, PACK, width], F32, name="y_sb")
+            per_bank = 512 // width
+            for s0 in range(0, PACK, per_bank):
+                bank = psum.tile([P, per_bank, width], F32, name="score")
+                for s in range(s0, s0 + per_bank):
+                    for b in range(2):
+                        score_pass(bank[:, s - s0, :], s, b, js, b == 0, b == 1)
+                for s in range(s0, s0 + per_bank):
+                    nc.scalar.activation(out=y_sb[j0][:, s, :], in_=bank[:, s - s0, :], func=ACT.Identity,
+                                         bias=base_sb[:, s : s + 1])
+            nc.sync.dma_start(out=y_rows[:, :, js], in_=y_sb[j0][:])
+
+        def round_y(j0, width, engine):
+            y_bf[j0] = work.tile([P, width * PACK], BF16, name="y_bf", align_bytes=64)
+            dst = y_bf[j0][:].rearrange("p (c i s) -> p c s i", i=4, s=PACK)
+            src = y_sb[j0][:].rearrange("p s (c i) -> p c s i", i=4)
+            for c0 in range(0, width // 4, 32):
+                if engine == "scalar":
+                    nc.scalar.copy(out=dst[:, c0 : c0 + 32], in_=src[:, c0 : c0 + 32])
+                else:
+                    nc.vector.tensor_copy(out=dst[:, c0 : c0 + 32], in_=src[:, c0 : c0 + 32])
+
+        def quantize_y(j0, width):
+            js = slice(j0, j0 + width)
+            nc.vector.quantize_mx(out=y_w[:, js].bitcast(FP8X4), scales=y_s[:, js], in_=y_bf[j0][:])
+            nc.sync.dma_start(out=y_w_dst[:, js], in_=y_w[:, js].bitcast(I32))
+
+        nc.sync.dma_start(offsets[:], offs)
+        nc.vector.memset(tab_s[:].bitcast(I32), 0)
+        for q in range(QUADS):
+            nc.scalar.dma_start(out=wab_s_raw[32 * q + WB_ROW : 32 * q + WB_ROW + 4, :].bitcast(I32),
+                                in_=wb_scales[0, 4 * q : 4 * q + 4, :].bitcast(I32))
+        load_wab(0)
+        load_wq(0)
+        nc.sync.dma_start(out=tab_w[:].bitcast(I32), in_=tab_words[0].rearrange("p t i -> p (t i)").bitcast(I32))
+        for q in range(QUADS):
+            nc.scalar.dma_start(out=tab_s[32 * q : 32 * q + 4, :].bitcast(I32), in_=tab_scales[0, 4 * q : 4 * q + 4, :].bitcast(I32))
+        for q in range(QUADS):
+            nc.gpsimd.dma_start(out=wab_s_raw[32 * q : 32 * q + 4, :].bitcast(I32), in_=wa_scales[0, 4 * q : 4 * q + 4, :].bitcast(I32))
+        nc.gpsimd.dma_start(out=base_sb[:], in_=base.rearrange("(p s) -> p s", s=PACK))
+        nc.vector.memset(wab_s[:].bitcast(I32), 0)
+        for t in range(PACK):
+            round_wq(0, t)
+        deal_wab(0)
+        load_wab(1)
+        load_wq(1)
+        nc.vector.tensor_copy(out=v_s[:], in_=tab_s[:].indirect(offsets[:]))
+        quantize_w("wq", 0)
+        for q in range(QUADS):
+            rows = slice(32 * q, 32 * q + 2 * WB_ROW)
+            nc.vector.tensor_copy(
+                out=wab_s[rows, :].bitcast(I32).rearrange("p (b t q i) -> p b t q i", b=2, t=PACK, q=BLOCKS),
+                in_=wab_s_raw[rows, :].bitcast(I32).rearrange("p (b q t i) -> p b t q i", b=2, t=PACK, q=BLOCKS),
+            )
+        gather_words(0, 256)
+        gather_words(256, 512)
+
+        units = [(0, c) for c in range(4)] + [(1, c) for c in range(4)]
+        units = units + [(0, 4), (0, 5), (1, 4), (1, 5), (0, 6), (1, 6), (0, 7), (1, 7)]
+
+        def last_open():
+            js = slice(S - CHUNK, S)
+            banks["last"] = psum.tile([P, PACK, CHUNK], F32, name="score")
+            for s in range(PACK):
+                score_pass(banks["last"][:, s, :], s, 0, js, s == 0, False)
+
+        beside = {
+            0: [lambda: round_wq(1, 0), lambda: round_wq(1, 1)],
+            1: [lambda: round_wq(1, 2), lambda: round_wq(1, 3)],
+            2: [lambda: quantize_w("wq", 1), lambda: round_ws(0, 0), lambda: round_ws(0, 1)],
+            3: [lambda: round_ws(0, 2), lambda: round_ws(0, 3)],
+            4: [lambda: quantize_w("ws", 0), lambda: round_ws(1, 0), lambda: round_ws(1, 1)],
+            5: [lambda: round_ws(1, 2), lambda: round_ws(1, 3)],
+            6: [lambda: quantize_w("ws", 1)],
+            7: [lambda: score(0, 256)],
+            8: [lambda: round_y(0, 256, "scalar")],
+            9: [lambda: quantize_y(0, 256), lambda: score(256, 256)],
+            10: [lambda: round_y(256, 256, "scalar")],
+            11: [lambda: quantize_y(256, 256)],
+            12: [lambda: score(512, 256)],
+            13: [lambda: round_y(512, 256, "scalar")],
+            14: [lambda: quantize_y(512, 256), lambda: score(768, 128)],
+            15: [lambda: round_y(768, 128, "scalar"), last_open],
+        }
+
+        products(units[0])
+        gather_words(512, 1024)
+        deal_wab(1)
+        load_ws(0)
+        load_ws(1)
+        for u, unit in enumerate(units):
+            if u + 1 < len(units):
+                products(units[u + 1])
+            weigh(unit, 0)
+            if u > 0:
+                join(units[u - 1])
+            weigh(unit, 1)
+            if u > 0:
+                quantize_h(units[u - 1])
+            for step in beside[u]:
+                step()
+        join(units[-1])
+        quantize_y(768, 128)
+        quantize_h(units[-1])
+
+        j0 = S - CHUNK
+        js = slice(j0, S)
+        bank = banks["last"]
+        for s in range(PACK):
+            score_pass(bank[:, s, :], s, 1, js, False, s == PACK - 1)
+        y_sb[j0] = work.tile([P, PACK, CHUNK], F32, name="y_sb")
+        nc.vector.tensor_tensor(out=y_sb[j0][:], in0=bank[:], in1=base_sb[:].unsqueeze(2).to_broadcast([P, PACK, CHUNK]), op=ALU.add)
+        nc.sync.dma_start(out=y_rows[:, :, js], in_=y_sb[j0][:])
+        round_y(j0, CHUNK, "vector")
+        quantize_y(j0, CHUNK)
+        for q in range(QUADS):
+            engine = nc.scalar if q % 2 else nc.sync
+            engine.dma_start(out=out_2[0, 4 * q : 4 * q + 4, :].bitcast(I32), in_=y_s[32 * q : 32 * q + 4, :].bitcast(I32))

@@ -35,6 +35,7 @@ def tile_list_routed_credit_scorecard_kernel(
         wq_stage = ctx.enter_context(tc.tile_pool(name="wq_stage", bufs=1))
         ring = ctx.enter_context(tc.tile_pool(name="ring", bufs=2))
         work = ctx.enter_context(tc.tile_pool(name="work", bufs=2))
+        ahead = ctx.enter_context(tc.tile_pool(name="ahead", bufs=4))
         psum = ctx.enter_context(tc.psum_pool(name="psum", bufs=2))
 
         offsets = keep.tile([P, S // 16], U16, name="offsets")
@@ -94,17 +95,18 @@ def tile_list_routed_credit_scorecard_kernel(
         def round_wq(b, t):
             if t == 0:
                 rounded["wq", b] = work.tile([P, PASS * PACK], BF16, name="w_bf", tag="w_bf", align_bytes=64)
-            dst = rounded["wq", b][:].rearrange("p (t q i j) -> p t q j i", t=PACK, q=BLOCKS, j=PACK)
-            src = raw["wq", b][:].rearrange("p j (q t i) -> p t q j i", t=PACK, i=RUN)
-            nc.scalar.activation(out=dst[:, t], in_=src[:, t], func=ACT.Identity)
+            dst = rounded["wq", b][:].rearrange("p (t q h i j) -> p t h q j i", t=PACK, q=BLOCKS, h=2, j=PACK)
+            src = raw["wq", b][:].rearrange("p j (q t h i) -> p t h q j i", t=PACK, h=2, i=RUN // 2)
+            for h in range(2):
+                nc.scalar.activation(out=dst[:, t, h], in_=src[:, t, h], func=ACT.Identity)
 
         def round_ws(b, part):
             if part == 0:
                 rounded["ws", b] = work.tile([P, N * PACK], BF16, name="w_bf", tag="w_bf", align_bytes=64)
-            ms = slice(32 * part, 32 * (part + 1))
-            dst = rounded["ws", b][:].rearrange("p (s m t) -> p m t s", s=PACK, t=PACK)
-            src = raw["ws", b][:].rearrange("p t (m s) -> p m t s", s=PACK)
-            nc.scalar.activation(out=dst[:, ms], in_=src[:, ms], func=ACT.Identity)
+            ms = slice(64 * (part // 2), 64 * (part // 2 + 1))
+            dst = rounded["ws", b][:].rearrange("p (u e m t) -> p u m t e", u=2, e=2, t=PACK)
+            src = raw["ws", b][:].rearrange("p t (m u e) -> p u m t e", u=2, e=2)
+            nc.scalar.activation(out=dst[:, part % 2, ms], in_=src[:, part % 2, ms], func=ACT.Identity)
 
         def quantize_w(kind, b):
             words, scales = (wq_w, wq_s) if kind == "wq" else (ws_w, ws_s)
@@ -117,53 +119,56 @@ def tile_list_routed_credit_scorecard_kernel(
         halves = {}
         h_bf = {}
 
-        def products(unit):
-            b, c = unit
-            js = slice(CHUNK * c, CHUNK * (c + 1))
-            route = psum.tile([P, PACK, CHUNK], F32, name="route")
-            left = psum.tile([P, PACK, CHUNK], F32, name="left")
-            right = psum.tile([P, PACK, CHUNK], F32, name="right")
-            moving = dict_moving(js)
-            for t in range(PACK):
-                cols = slice(P * t, P * (t + 1))
-                nc.tensor.matmul_mx(out=route[:, t, :], lhsT=wq_w[b][:, cols].bitcast(FP8X4), lhsT_scale=wq_s[b][:, cols],
-                                    rhs=moving[0], rhs_scale=moving[1], start=True, stop=True)
-            route_sb = work.tile([P, CHUNK, PACK], F32, name="route_sb")
-            nc.scalar.copy(out=route_sb[:], in_=route[:].rearrange("p t n -> p n t"))
-            for t in range(PACK):
-                scols = slice(PASS * b + P * t, PASS * b + P * (t + 1))
-                nc.tensor.matmul_mx(out=left[:, t, :], lhsT=wa_w[b][:, 2 * P * t : 2 * P * (t + 1)].bitcast(FP4X4),
-                                    lhsT_scale=wab_s[:, scols], rhs=moving[0], rhs_scale=moving[1], start=True, stop=True)
-            for t in range(PACK):
-                cols = slice(P * t, P * (t + 1))
-                scols = slice(PASS * b + P * t, PASS * b + P * (t + 1))
-                nc.tensor.matmul_mx(out=right[:, t, :], lhsT=wb_w[b][:, cols].bitcast(FP8X4),
-                                    lhsT_scale=wab_s[WB_ROW:P, scols], rhs=moving[0], rhs_scale=moving[1], start=True, stop=True)
-            banks[unit] = (route_sb, left, right)
+        def product(name, unit, stationary):
+            (b, j0, width), pair = unit
+            js = slice(j0, j0 + width)
+            bank = psum.tile([P, 2, width], F32, name=name)
+            for e in range(2):
+                words, scales = stationary(b, 2 * pair + e)
+                nc.tensor.matmul_mx(out=bank[:, e, :], lhsT=words, lhsT_scale=scales, rhs=v_w[:, js].bitcast(FP8X4),
+                                    rhs_scale=v_s[:, js], start=True, stop=True)
+            return bank[:].rearrange("p e n -> p n e")
 
-        def dict_moving(js):
-            return v_w[:, js].bitcast(FP8X4), v_s[:, js]
+        def wq_slot(b, t):
+            cols = slice(P * t, P * (t + 1))
+            return wq_w[b][:, cols].bitcast(FP8X4), wq_s[b][:, cols]
+
+        def wa_slot(b, t):
+            return wa_w[b][:, 2 * P * t : 2 * P * (t + 1)].bitcast(FP4X4), wab_s[:, PASS * b + P * t : PASS * b + P * (t + 1)]
+
+        def wb_slot(b, t):
+            return wb_w[b][:, P * t : P * (t + 1)].bitcast(FP8X4), wab_s[WB_ROW:P, PASS * b + P * t : PASS * b + P * (t + 1)]
+
+        def route_product(unit):
+            route = product("route", unit, wq_slot)
+            banks[unit, "route"] = ahead.tile([P, unit[0][2], 2], F32, name="route_sb")
+            nc.scalar.copy(out=banks[unit, "route"][:], in_=route)
+
+        def side_products(unit):
+            banks[unit, 0] = product("left", unit, wa_slot)
+            banks[unit, 1] = product("right", unit, wb_slot)
 
         def weigh(unit, side):
-            route_sb = banks[unit][0]
-            half = work.tile([P, CHUNK, PACK], BF16, name="half%d" % side, align_bytes=64)
+            group, pair = unit
+            if pair == 0:
+                halves[group, side] = work.tile([P, 2, group[2], 2], BF16, name="half%d" % side, align_bytes=64)
             nc.vector.scalar_tensor_tensor(
-                out=half[:], in0=route_sb[:], scalar=0.0, in1=banks[unit][1 + side][:].rearrange("p t n -> p n t"),
+                out=halves[group, side][:, pair], in0=banks[unit, "route"][:], scalar=0.0, in1=banks[unit, side],
                 op0=ALU.max if side == 0 else ALU.min, op1=ALU.mult,
             )
-            halves[unit, side] = half
 
-        def join(unit):
-            h_bf[unit] = work.tile([P, CHUNK * PACK], BF16, name="h_bf", align_bytes=64)
+        def join(group):
+            h_bf[group] = work.tile([P, group[2], 2, 2], BF16, name="h_bf", align_bytes=64)
             nc.vector.tensor_tensor(
-                out=h_bf[unit][:], in0=halves[unit, 0][:].rearrange("p n t -> p (n t)"),
-                in1=halves[unit, 1][:].rearrange("p n t -> p (n t)"), op=ALU.subtract,
+                out=h_bf[group][:], in0=halves[group, 0][:].rearrange("p u n e -> p n u e"),
+                in1=halves[group, 1][:].rearrange("p u n e -> p n u e"), op=ALU.subtract,
             )
 
-        def quantize_h(unit):
-            b, c = unit
-            js = slice(CHUNK * c, CHUNK * (c + 1))
-            nc.vector.quantize_mx(out=h_w[b][:, js].bitcast(FP8X4), scales=h_s[b][:, js], in_=h_bf[unit][:])
+        def quantize_h(group):
+            b, j0, width = group
+            js = slice(j0, j0 + width)
+            nc.vector.quantize_mx(out=h_w[b][:, js].bitcast(FP8X4), scales=h_s[b][:, js],
+                                  in_=h_bf[group][:].rearrange("p n u e -> p (n u e)"))
 
         y_sb = {}
         y_bf = {}
@@ -173,19 +178,20 @@ def tile_list_routed_credit_scorecard_kernel(
             nc.tensor.matmul_mx(out=bank, lhsT=ws_w[b][:, cols].bitcast(FP8X4), lhsT_scale=ws_s[b][:, cols],
                                 rhs=h_w[b][:, js].bitcast(FP8X4), rhs_scale=h_s[b][:, js], start=start, stop=stop)
 
-        def score(j0, width):
+        def score(j0, width, s0):
             js = slice(j0, j0 + width)
-            y_sb[j0] = work.tile([P, PACK, width], F32, name="y_sb")
+            if s0 == 0:
+                y_sb[j0] = work.tile([P, PACK, width], F32, name="y_sb")
             per_bank = 512 // width
-            for s0 in range(0, PACK, per_bank):
-                bank = psum.tile([P, per_bank, width], F32, name="score")
-                for s in range(s0, s0 + per_bank):
-                    for b in range(2):
-                        score_pass(bank[:, s - s0, :], s, b, js, b == 0, b == 1)
-                for s in range(s0, s0 + per_bank):
-                    nc.scalar.activation(out=y_sb[j0][:, s, :], in_=bank[:, s - s0, :], func=ACT.Identity,
-                                         bias=base_sb[:, s : s + 1])
-            nc.sync.dma_start(out=y_rows[:, :, js], in_=y_sb[j0][:])
+            bank = psum.tile([P, per_bank, width], F32, name="score")
+            for s in range(s0, s0 + per_bank):
+                for b in range(2):
+                    score_pass(bank[:, s - s0, :], s, b, js, b == 0, b == 1)
+            for s in range(s0, s0 + per_bank):
+                nc.scalar.activation(out=y_sb[j0][:, s, :], in_=bank[:, s - s0, :], func=ACT.Identity,
+                                     bias=base_sb[:, s : s + 1])
+            if s0 + per_bank == PACK:
+                nc.sync.dma_start(out=y_rows[:, :, js], in_=y_sb[j0][:])
 
         def round_y(j0, width, engine):
             y_bf[j0] = work.tile([P, width * PACK], BF16, name="y_bf", align_bytes=64)
@@ -204,9 +210,7 @@ def tile_list_routed_credit_scorecard_kernel(
 
         nc.sync.dma_start(offsets[:], offs)
         nc.vector.memset(tab_s[:].bitcast(I32), 0)
-        for q in range(QUADS):
-            nc.scalar.dma_start(out=wab_s_raw[32 * q + WB_ROW : 32 * q + WB_ROW + 4, :].bitcast(I32),
-                                in_=wb_scales[0, 4 * q : 4 * q + 4, :].bitcast(I32))
+        nc.vector.memset(wab_s_raw[:].bitcast(I32), 0)
         load_wab(0)
         load_wq(0)
         nc.sync.dma_start(out=tab_w[:].bitcast(I32), in_=tab_words[0].rearrange("p t i -> p (t i)").bitcast(I32))
@@ -214,8 +218,11 @@ def tile_list_routed_credit_scorecard_kernel(
             nc.scalar.dma_start(out=tab_s[32 * q : 32 * q + 4, :].bitcast(I32), in_=tab_scales[0, 4 * q : 4 * q + 4, :].bitcast(I32))
         for q in range(QUADS):
             nc.gpsimd.dma_start(out=wab_s_raw[32 * q : 32 * q + 4, :].bitcast(I32), in_=wa_scales[0, 4 * q : 4 * q + 4, :].bitcast(I32))
+        for q in range(QUADS):
+            queue = nc.scalar if q < QUADS - 1 else nc.gpsimd
+            queue.dma_start(out=wab_s_raw[32 * q + WB_ROW : 32 * q + WB_ROW + 4, :].bitcast(I32),
+                            in_=wb_scales[0, 4 * q : 4 * q + 4, :].bitcast(I32))
         nc.gpsimd.dma_start(out=base_sb[:], in_=base.rearrange("(p s) -> p s", s=PACK))
-        nc.vector.memset(wab_s[:].bitcast(I32), 0)
         for t in range(PACK):
             round_wq(0, t)
         deal_wab(0)
@@ -223,17 +230,16 @@ def tile_list_routed_credit_scorecard_kernel(
         load_wq(1)
         nc.vector.tensor_copy(out=v_s[:], in_=tab_s[:].indirect(offsets[:]))
         quantize_w("wq", 0)
-        for q in range(QUADS):
-            rows = slice(32 * q, 32 * q + 2 * WB_ROW)
-            nc.vector.tensor_copy(
-                out=wab_s[rows, :].bitcast(I32).rearrange("p (b t q i) -> p b t q i", b=2, t=PACK, q=BLOCKS),
-                in_=wab_s_raw[rows, :].bitcast(I32).rearrange("p (b q t i) -> p b t q i", b=2, t=PACK, q=BLOCKS),
-            )
+        nc.vector.tensor_copy(
+            out=wab_s[:].bitcast(I32).rearrange("p (b t q i) -> p b t q i", b=2, t=PACK, q=BLOCKS),
+            in_=wab_s_raw[:].bitcast(I32).rearrange("p (b q t i) -> p b t q i", b=2, t=PACK, q=BLOCKS),
+        )
         gather_words(0, 256)
         gather_words(256, 512)
 
-        units = [(0, c) for c in range(4)] + [(1, c) for c in range(4)]
-        units = units + [(0, 4), (0, 5), (1, 4), (1, 5), (0, 6), (1, 6), (0, 7), (1, 7)]
+        groups = [(0, 0, 256), (0, 256, 256), (1, 0, 256), (1, 256, 256), (0, 512, 256), (1, 512, 256),
+                  (0, 768, 256), (1, 768, 128), (1, 896, 128)]
+        units = [(group, pair) for group in groups for pair in range(2)]
 
         def last_open():
             js = slice(S - CHUNK, S)
@@ -242,43 +248,52 @@ def tile_list_routed_credit_scorecard_kernel(
                 score_pass(banks["last"][:, s, :], s, 0, js, s == 0, False)
 
         beside = {
-            0: [lambda: round_wq(1, 0), lambda: round_wq(1, 1)],
-            1: [lambda: round_wq(1, 2), lambda: round_wq(1, 3)],
-            2: [lambda: quantize_w("wq", 1), lambda: round_ws(0, 0), lambda: round_ws(0, 1)],
+            0: [lambda: round_wq(1, 2), lambda: round_wq(1, 3)],
+            1: [lambda: quantize_w("wq", 1)],
+            2: [lambda: round_ws(0, 0), lambda: round_ws(0, 1)],
             3: [lambda: round_ws(0, 2), lambda: round_ws(0, 3)],
             4: [lambda: quantize_w("ws", 0), lambda: round_ws(1, 0), lambda: round_ws(1, 1)],
             5: [lambda: round_ws(1, 2), lambda: round_ws(1, 3)],
-            6: [lambda: quantize_w("ws", 1)],
-            7: [lambda: score(0, 256)],
+            6: [lambda: quantize_w("ws", 1), lambda: score(0, 256, 0)],
+            7: [lambda: score(0, 256, 2)],
             8: [lambda: round_y(0, 256, "scalar")],
-            9: [lambda: quantize_y(0, 256), lambda: score(256, 256)],
+            9: [lambda: quantize_y(0, 256), lambda: score(256, 256, 0), lambda: score(256, 256, 2)],
             10: [lambda: round_y(256, 256, "scalar")],
             11: [lambda: quantize_y(256, 256)],
-            12: [lambda: score(512, 256)],
+            12: [lambda: score(512, 256, 0), lambda: score(512, 256, 2)],
             13: [lambda: round_y(512, 256, "scalar")],
-            14: [lambda: quantize_y(512, 256), lambda: score(768, 128)],
-            15: [lambda: round_y(768, 128, "scalar"), last_open],
+            14: [lambda: quantize_y(512, 256)],
+            15: [],
+            16: [lambda: score(768, 128, 0), last_open, lambda: round_y(768, 128, "scalar")],
+            17: [],
         }
 
-        products(units[0])
+        route_product(units[0])
+        side_products(units[0])
+        route_product(units[1])
         gather_words(512, 1024)
         deal_wab(1)
         load_ws(0)
         load_ws(1)
+        round_wq(1, 0)
+        round_wq(1, 1)
         for u, unit in enumerate(units):
+            if u + 2 < len(units):
+                route_product(units[u + 2])
             if u + 1 < len(units):
-                products(units[u + 1])
+                side_products(units[u + 1])
+            done = units[u - 1][0] if u > 0 and unit[1] == 0 else None
             weigh(unit, 0)
-            if u > 0:
-                join(units[u - 1])
+            if done:
+                join(done)
             weigh(unit, 1)
-            if u > 0:
-                quantize_h(units[u - 1])
+            if done:
+                quantize_h(done)
             for step in beside[u]:
                 step()
-        join(units[-1])
+        join(groups[-1])
+        quantize_h(groups[-1])
         quantize_y(768, 128)
-        quantize_h(units[-1])
 
         j0 = S - CHUNK
         js = slice(j0, S)

@@ -32,8 +32,7 @@ def tile_list_routed_credit_scorecard_kernel(
     nc = tc.nc
     with ExitStack() as ctx:
         keep = ctx.enter_context(tc.tile_pool(name="keep", bufs=1))
-        wq_stage = ctx.enter_context(tc.tile_pool(name="wq_stage", bufs=1))
-        ring = ctx.enter_context(tc.tile_pool(name="ring", bufs=2))
+        stage = ctx.enter_context(tc.tile_pool(name="stage", bufs=1))
         work = ctx.enter_context(tc.tile_pool(name="work", bufs=2))
         ahead = ctx.enter_context(tc.tile_pool(name="ahead", bufs=4))
         psum = ctx.enter_context(tc.psum_pool(name="psum", bufs=2))
@@ -41,15 +40,18 @@ def tile_list_routed_credit_scorecard_kernel(
         offsets = keep.tile([P, S // 16], U16, name="offsets")
         tab_w = keep.tile([P, T], U32, name="tab_w", align_bytes=64)
         tab_s = keep.tile([P, T], U8, name="tab_s", align_bytes=64)
+        tab_s_raw = stage.tile([P, T], U8, name="tab_s_raw", tag="c", align_bytes=64)
         v_w = keep.tile([P, S], U32, name="v_w", align_bytes=64)
         v_s = keep.tile([P, S], U8, name="v_s", align_bytes=64)
-        wab_s_raw = keep.tile([P, H], U8, name="wab_s_raw", align_bytes=64)
-        wab_s = keep.tile([P, H], U8, name="wab_s", align_bytes=64)
+        wa_s_raw = keep.tile([P, H], U8, name="wa_s_raw", align_bytes=64)
+        wb_s_raw = keep.tile([P, H], U8, name="wb_s_raw", align_bytes=64)
+        wa_s = keep.tile([P, H], U8, name="wa_s", align_bytes=64)
+        wb_s = keep.tile([P, H], U8, name="wb_s", align_bytes=64)
         base_sb = keep.tile([P, PACK], F32, name="base_sb")
         wq_w = [keep.tile([P, PASS], U32, name="wq_w%d" % b, align_bytes=64) for b in range(2)]
         wq_s = [keep.tile([P, PASS], U8, name="wq_s%d" % b, align_bytes=64) for b in range(2)]
-        wa_w = [keep.tile([P, 2 * PASS], U8, name="wa_w%d" % b, align_bytes=64) for b in range(2)]
-        wb_w = [keep.tile([P, PASS], U32, name="wb_w%d" % b, align_bytes=64) for b in range(2)]
+        wa_w = {}
+        wb_w = {}
         ws_w = [keep.tile([P, N], U32, name="ws_w%d" % b, align_bytes=64) for b in range(2)]
         ws_s = [keep.tile([P, N], U8, name="ws_s%d" % b, align_bytes=64) for b in range(2)]
         h_w = [keep.tile([P, S], U32, name="h_w%d" % b, align_bytes=64) for b in range(2)]
@@ -67,34 +69,49 @@ def tile_list_routed_credit_scorecard_kernel(
         rounded = {}
 
         def load_wq(b):
-            raw["wq", b] = wq_stage.tile([P, PACK, PASS], F32, name="wq_raw")
+            raw["wq", b] = stage.tile([P, PACK, PASS], F32, name="wq_raw", tag="ac"[b], align_bytes=64)
             nc.sync.dma_start(out=raw["wq", b][:], in_=wq_rows[:, :, PASS * b : PASS * (b + 1)])
 
         def load_wab(b):
-            raw["wa", b] = ring.tile([P, PASS // 2], I32, name="wa_raw", tag="ring")
-            nc.sync.dma_start(out=raw["wa", b][:], in_=wa_src[:, PASS // 2 * b : PASS // 2 * (b + 1)])
-            raw["wb", b] = ring.tile([P, PASS], I32, name="wb_raw", tag="ring")
-            nc.sync.dma_start(out=raw["wb", b][:], in_=wb_src[:, PASS * b : PASS * (b + 1)])
+            both = stage.tile([P, PASS // 2 + PASS], I32, name="wab_raw", tag="d", align_bytes=64)
+            raw["wa", b] = both[:, 0 : PASS // 2]
+            raw["wb", b] = both[:, PASS // 2 : PASS // 2 + PASS]
+            nc.sync.dma_start(out=raw["wa", b], in_=wa_src[:, PASS // 2 * b : PASS // 2 * (b + 1)])
+            nc.sync.dma_start(out=raw["wb", b], in_=wb_src[:, PASS * b : PASS * (b + 1)])
 
         def load_ws(b):
-            raw["ws", b] = ring.tile([P, PACK, N], F32, name="ws_raw", tag="ring")
+            raw["ws", b] = stage.tile([P, PACK, N], F32, name="ws_raw", tag="ab"[b], align_bytes=64)
             rows = ws[PASS * b : PASS * (b + 1), :].rearrange("(q t i) n -> t q i n", t=PACK, i=RUN)
             for t in range(PACK):
                 nc.sync.dma_start(out=raw["ws", b][:, t, :], in_=rows[t])
 
         def deal_wab(b):
-            nc.vector.tensor_copy(
-                out=wa_w[b][:].bitcast(I32).rearrange("p (t q i) -> p t q i", t=PACK, q=BLOCKS),
-                in_=raw["wa", b][:].rearrange("p (q t i) -> p t q i", t=PACK, q=BLOCKS),
+            both = stage.tile([P, PASS // 2 + PASS], U32, name="wab_w", tag=("w", "g")[b], align_bytes=64)
+            wa_w[b] = both[:, 0 : PASS // 2]
+            wb_w[b] = both[:, PASS // 2 : PASS // 2 + PASS]
+            nc.scalar.copy(
+                out=wa_w[b].rearrange("p (t q i) -> p t q i", t=PACK, q=BLOCKS),
+                in_=raw["wa", b].bitcast(U32).rearrange("p (q t i) -> p t q i", t=PACK, q=BLOCKS),
             )
-            nc.vector.tensor_copy(
-                out=wb_w[b][:].bitcast(I32).rearrange("p (t q i) -> p t q i", t=PACK, q=BLOCKS),
-                in_=raw["wb", b][:].rearrange("p (q t i) -> p t q i", t=PACK, q=BLOCKS),
+            nc.scalar.copy(
+                out=wb_w[b].rearrange("p (t q i) -> p t q i", t=PACK, q=BLOCKS),
+                in_=raw["wb", b].bitcast(U32).rearrange("p (q t i) -> p t q i", t=PACK, q=BLOCKS),
             )
 
+        def deal_scales(dst, src, b):
+            cols = slice(PASS * b, PASS * (b + 1))
+            for q in range(QUADS):
+                rows = slice(32 * q, 32 * q + 4)
+                nc.scalar.copy(
+                    out=dst[rows, cols].bitcast(U32).rearrange("p (t q i) -> p t q i", t=PACK, q=BLOCKS),
+                    in_=src[rows, cols].bitcast(U32).rearrange("p (q t i) -> p t q i", t=PACK, q=BLOCKS),
+                )
+
         def round_wq(b, t):
-            if t == 0:
-                rounded["wq", b] = work.tile([P, PASS * PACK], BF16, name="w_bf", tag="w_bf", align_bytes=64)
+            if t == 0 and b == 0:
+                rounded["wq", b] = stage.tile([P, PASS * PACK], BF16, name="w_bf", tag="b", align_bytes=64)
+            elif t == 0:
+                rounded["wq", b] = stage.tile([P, PASS * PACK], BF16, name="w_bf", tag="e", align_bytes=64)
             dst = rounded["wq", b][:].rearrange("p (t q h i j) -> p t h q j i", t=PACK, q=BLOCKS, h=2, j=PACK)
             src = raw["wq", b][:].rearrange("p j (q t h i) -> p t h q j i", t=PACK, h=2, i=RUN // 2)
             for h in range(2):
@@ -102,7 +119,7 @@ def tile_list_routed_credit_scorecard_kernel(
 
         def round_ws(b, part):
             if part == 0:
-                rounded["ws", b] = work.tile([P, N * PACK], BF16, name="w_bf", tag="w_bf", align_bytes=64)
+                rounded["ws", b] = stage.tile([P, N * PACK], BF16, name="w_bf", tag="fe"[b], align_bytes=64)
             ms = slice(64 * (part // 2), 64 * (part // 2 + 1))
             dst = rounded["ws", b][:].rearrange("p (u e m t) -> p u m t e", u=2, e=2, t=PACK)
             src = raw["ws", b][:].rearrange("p t (m u e) -> p u m t e", u=2, e=2)
@@ -134,14 +151,17 @@ def tile_list_routed_credit_scorecard_kernel(
             return wq_w[b][:, cols].bitcast(FP8X4), wq_s[b][:, cols]
 
         def wa_slot(b, t):
-            return wa_w[b][:, 2 * P * t : 2 * P * (t + 1)].bitcast(FP4X4), wab_s[:, PASS * b + P * t : PASS * b + P * (t + 1)]
+            return wa_w[b][:, P // 2 * t : P // 2 * (t + 1)].bitcast(FP4X4), wa_s[:, PASS * b + P * t : PASS * b + P * (t + 1)]
 
         def wb_slot(b, t):
-            return wb_w[b][:, P * t : P * (t + 1)].bitcast(FP8X4), wab_s[WB_ROW:P, PASS * b + P * t : PASS * b + P * (t + 1)]
+            return wb_w[b][:, P * t : P * (t + 1)].bitcast(FP8X4), wb_s[:, PASS * b + P * t : PASS * b + P * (t + 1)]
 
         def route_product(unit):
             route = product("route", unit, wq_slot)
-            banks[unit, "route"] = ahead.tile([P, unit[0][2], 2], F32, name="route_sb")
+            if unit in units[:3]:
+                banks[unit, "route"] = stage.tile([P, unit[0][2], 2], F32, name="route_sb", tag="egf"[units.index(unit)], align_bytes=64)
+            else:
+                banks[unit, "route"] = ahead.tile([P, unit[0][2], 2], F32, name="route_sb")
             nc.scalar.copy(out=banks[unit, "route"][:], in_=route)
 
         def side_products(unit):
@@ -208,36 +228,41 @@ def tile_list_routed_credit_scorecard_kernel(
             nc.vector.quantize_mx(out=y_w[:, js].bitcast(FP8X4), scales=y_s[:, js], in_=y_bf[j0][:])
             nc.sync.dma_start(out=y_w_dst[:, js], in_=y_w[:, js].bitcast(I32))
 
-        nc.sync.dma_start(offsets[:], offs)
+        def load_scale_rows(tile, row0, src, q):
+            nc.sync.dma_start(out=tile[32 * q + row0 : 32 * q + row0 + 4, :].bitcast(I32), in_=src[0, 4 * q : 4 * q + 4, :].bitcast(I32))
+
         nc.vector.memset(tab_s[:].bitcast(I32), 0)
-        nc.vector.memset(wab_s_raw[:].bitcast(I32), 0)
+        nc.vector.memset(wa_s[:].bitcast(I32), 0)
+        nc.vector.memset(wb_s[:].bitcast(I32), 0)
+        nc.sync.dma_start(offsets[:], offs)
+        for q in range(QUADS):
+            load_scale_rows(tab_s_raw, 0, tab_scales, q)
         load_wab(0)
         load_wq(0)
+        for q in range(QUADS):
+            load_scale_rows(wa_s_raw, 0, wa_scales, q)
         nc.sync.dma_start(out=tab_w[:].bitcast(I32), in_=tab_words[0].rearrange("p t i -> p (t i)").bitcast(I32))
         for q in range(QUADS):
-            nc.scalar.dma_start(out=tab_s[32 * q : 32 * q + 4, :].bitcast(I32), in_=tab_scales[0, 4 * q : 4 * q + 4, :].bitcast(I32))
-        for q in range(QUADS):
-            nc.gpsimd.dma_start(out=wab_s_raw[32 * q : 32 * q + 4, :].bitcast(I32), in_=wa_scales[0, 4 * q : 4 * q + 4, :].bitcast(I32))
-        for q in range(QUADS):
-            queue = nc.scalar if q < QUADS - 1 else nc.gpsimd
-            queue.dma_start(out=wab_s_raw[32 * q + WB_ROW : 32 * q + WB_ROW + 4, :].bitcast(I32),
-                            in_=wb_scales[0, 4 * q : 4 * q + 4, :].bitcast(I32))
+            load_scale_rows(wb_s_raw, 0, wb_scales, q)
         nc.gpsimd.dma_start(out=base_sb[:], in_=base.rearrange("(p s) -> p s", s=PACK))
-        for t in range(PACK):
-            round_wq(0, t)
         deal_wab(0)
         load_wab(1)
-        load_wq(1)
+        for t in range(PACK):
+            round_wq(0, t)
+        for q in range(QUADS):
+            nc.vector.tensor_copy(out=tab_s[32 * q : 32 * q + 4, :].bitcast(I32), in_=tab_s_raw[32 * q : 32 * q + 4, :].bitcast(I32))
         nc.vector.tensor_copy(out=v_s[:], in_=tab_s[:].indirect(offsets[:]))
+        deal_scales(wa_s, wa_s_raw, 0)
+        deal_scales(wa_s, wa_s_raw, 1)
+        deal_scales(wb_s, wb_s_raw, 0)
+        load_wq(1)
+        load_ws(0)
         quantize_w("wq", 0)
-        nc.vector.tensor_copy(
-            out=wab_s[:].bitcast(I32).rearrange("p (b t q i) -> p b t q i", b=2, t=PACK, q=BLOCKS),
-            in_=wab_s_raw[:].bitcast(I32).rearrange("p (b q t i) -> p b t q i", b=2, t=PACK, q=BLOCKS),
-        )
+        load_ws(1)
         gather_words(0, 256)
         gather_words(256, 512)
 
-        groups = [(0, 0, 256), (0, 256, 256), (1, 0, 256), (1, 256, 256), (0, 512, 256), (1, 512, 256),
+        groups = [(0, 0, 256), (0, 256, 256), (0, 512, 256), (1, 0, 256), (1, 256, 256), (1, 512, 256),
                   (0, 768, 256), (1, 768, 128), (1, 896, 128)]
         units = [(group, pair) for group in groups for pair in range(2)]
 
@@ -248,22 +273,22 @@ def tile_list_routed_credit_scorecard_kernel(
                 score_pass(banks["last"][:, s, :], s, 0, js, s == 0, False)
 
         beside = {
-            0: [lambda: round_wq(1, 2), lambda: round_wq(1, 3)],
-            1: [lambda: quantize_w("wq", 1)],
-            2: [lambda: round_ws(0, 0), lambda: round_ws(0, 1)],
-            3: [lambda: round_ws(0, 2), lambda: round_ws(0, 3)],
-            4: [lambda: quantize_w("ws", 0), lambda: round_ws(1, 0), lambda: round_ws(1, 1)],
-            5: [lambda: round_ws(1, 2), lambda: round_ws(1, 3)],
-            6: [lambda: quantize_w("ws", 1), lambda: score(0, 256, 0)],
-            7: [lambda: score(0, 256, 2)],
-            8: [lambda: round_y(0, 256, "scalar")],
-            9: [lambda: quantize_y(0, 256), lambda: score(256, 256, 0), lambda: score(256, 256, 2)],
-            10: [lambda: round_y(256, 256, "scalar")],
-            11: [lambda: quantize_y(256, 256)],
+            0: [lambda: round_wq(1, 0), lambda: round_wq(1, 1)],
+            1: [lambda: round_wq(1, 2), lambda: round_wq(1, 3)],
+            2: [lambda: deal_wab(1), lambda: deal_scales(wb_s, wb_s_raw, 1)],
+            3: [lambda: quantize_w("wq", 1), lambda: round_ws(0, 0), lambda: round_ws(0, 1)],
+            4: [lambda: round_ws(0, 2), lambda: round_ws(0, 3)],
+            5: [lambda: quantize_w("ws", 0), lambda: round_ws(1, 0), lambda: round_ws(1, 1)],
+            6: [lambda: round_ws(1, 2), lambda: round_ws(1, 3)],
+            7: [lambda: quantize_w("ws", 1)],
+            8: [lambda: score(0, 256, 0), lambda: score(0, 256, 2)],
+            9: [lambda: round_y(0, 256, "scalar")],
+            10: [lambda: score(256, 256, 0), lambda: score(256, 256, 2)],
+            11: [lambda: quantize_y(0, 256), lambda: round_y(256, 256, "scalar")],
             12: [lambda: score(512, 256, 0), lambda: score(512, 256, 2)],
-            13: [lambda: round_y(512, 256, "scalar")],
-            14: [lambda: quantize_y(512, 256)],
-            15: [],
+            13: [lambda: quantize_y(256, 256), lambda: round_y(512, 256, "scalar")],
+            14: [],
+            15: [lambda: quantize_y(512, 256)],
             16: [lambda: score(768, 128, 0), last_open, lambda: round_y(768, 128, "scalar")],
             17: [],
         }
@@ -272,11 +297,6 @@ def tile_list_routed_credit_scorecard_kernel(
         side_products(units[0])
         route_product(units[1])
         gather_words(512, 1024)
-        deal_wab(1)
-        load_ws(0)
-        load_ws(1)
-        round_wq(1, 0)
-        round_wq(1, 1)
         for u, unit in enumerate(units):
             if u + 2 < len(units):
                 route_product(units[u + 2])
@@ -300,11 +320,23 @@ def tile_list_routed_credit_scorecard_kernel(
         bank = banks["last"]
         for s in range(PACK):
             score_pass(bank[:, s, :], s, 1, js, False, s == PACK - 1)
-        y_sb[j0] = work.tile([P, PACK, CHUNK], F32, name="y_sb")
-        nc.vector.tensor_tensor(out=y_sb[j0][:], in0=bank[:], in1=base_sb[:].unsqueeze(2).to_broadcast([P, PACK, CHUNK]), op=ALU.add)
-        nc.sync.dma_start(out=y_rows[:, :, js], in_=y_sb[j0][:])
-        round_y(j0, CHUNK, "vector")
-        quantize_y(j0, CHUNK)
+        y_last = work.tile([P, PACK, CHUNK], F32, name="y_sb")
+        y_last_bf = work.tile([P, CHUNK * PACK], BF16, name="y_bf", align_bytes=64)
+        for half in range(2):
+            ns = slice(CHUNK // 2 * half, CHUNK // 2 * (half + 1))
+            nc.vector.tensor_tensor(out=y_last[:, :, ns], in0=bank[:, :, ns],
+                                    in1=base_sb[:].unsqueeze(2).to_broadcast([P, PACK, CHUNK // 2]), op=ALU.add)
+        nc.sync.dma_start(out=y_rows[:, :, js], in_=y_last[:])
+        for half in range(2):
+            es = slice(CHUNK * 2 * half, CHUNK * 2 * (half + 1))
+            ns = slice(CHUNK // 2 * half, CHUNK // 2 * (half + 1))
+            nc.vector.tensor_copy(out=y_last_bf[:, es].rearrange("p (c i s) -> p c s i", i=4, s=PACK),
+                                  in_=y_last[:, :, ns].rearrange("p s (c i) -> p c s i", i=4))
+        for half in range(2):
+            es = slice(CHUNK * 2 * half, CHUNK * 2 * (half + 1))
+            ns = slice(j0 + CHUNK // 2 * half, j0 + CHUNK // 2 * (half + 1))
+            nc.vector.quantize_mx(out=y_w[:, ns].bitcast(FP8X4), scales=y_s[:, ns], in_=y_last_bf[:, es])
+        nc.sync.dma_start(out=y_w_dst[:, js], in_=y_w[:, js].bitcast(I32))
         for q in range(QUADS):
             engine = nc.scalar if q % 2 else nc.sync
             engine.dma_start(out=out_2[0, 4 * q : 4 * q + 4, :].bitcast(I32), in_=y_s[32 * q : 32 * q + 4, :].bitcast(I32))

@@ -39,9 +39,10 @@ def tile_list_routed_credit_scorecard_kernel(
 
         offsets = keep.tile([P, S // 16], U16, name="offsets")
         tab_w = keep.tile([P, T], U32, name="tab_w", align_bytes=64)
-        tab_s = keep.tile([P, T], U8, name="tab_s", align_bytes=64)
-        tab_s_raw = stage.tile([P, T], U8, name="tab_s_raw", tag="c", align_bytes=64)
+        tab_s = stage.tile([P, T], U8, name="tab_s", tag="c", align_bytes=64)
+        tab_s_raw = keep.tile([P, T], U8, name="tab_s_raw", align_bytes=64)
         v_w = keep.tile([P, S], U32, name="v_w", align_bytes=64)
+        v_s_rows = keep.tile([P, S], U8, name="v_s_rows", align_bytes=64)
         v_s = keep.tile([P, S], U8, name="v_s", align_bytes=64)
         wa_s_raw = keep.tile([P, H], U8, name="wa_s_raw", align_bytes=64)
         wb_s_raw = keep.tile([P, H], U8, name="wb_s_raw", align_bytes=64)
@@ -98,13 +99,12 @@ def tile_list_routed_credit_scorecard_kernel(
                 in_=raw["wb", b].bitcast(U32).rearrange("p (q t i) -> p t q i", t=PACK, q=BLOCKS),
             )
 
-        def deal_scales(dst, src, b):
-            cols = slice(PASS * b, PASS * (b + 1))
+        def deal_scales(dst, src):
             for q in range(QUADS):
                 rows = slice(32 * q, 32 * q + 4)
                 nc.scalar.copy(
-                    out=dst[rows, cols].bitcast(U32).rearrange("p (t q i) -> p t q i", t=PACK, q=BLOCKS),
-                    in_=src[rows, cols].bitcast(U32).rearrange("p (q t i) -> p t q i", t=PACK, q=BLOCKS),
+                    out=dst[rows, :].bitcast(U32).rearrange("p (b t q i) -> p b t q i", b=2, t=PACK, q=BLOCKS),
+                    in_=src[rows, :].bitcast(U32).rearrange("p (b q t i) -> p b t q i", b=2, t=PACK, q=BLOCKS),
                 )
 
         def round_wq(b, t):
@@ -232,29 +232,31 @@ def tile_list_routed_credit_scorecard_kernel(
             nc.sync.dma_start(out=tile[32 * q + row0 : 32 * q + row0 + 4, :].bitcast(I32), in_=src[0, 4 * q : 4 * q + 4, :].bitcast(I32))
 
         nc.vector.memset(tab_s[:].bitcast(I32), 0)
+        nc.vector.memset(v_s[:].bitcast(I32), 0)
         nc.vector.memset(wa_s[:].bitcast(I32), 0)
         nc.vector.memset(wb_s[:].bitcast(I32), 0)
         nc.sync.dma_start(offsets[:], offs)
-        for q in range(QUADS):
-            load_scale_rows(tab_s_raw, 0, tab_scales, q)
+        nc.sync.dma_start(out=tab_s_raw[0:16, :].bitcast(I32), in_=tab_scales[0].bitcast(I32))
+        scale_rows = [(tile, src, q) for tile, src in ((wa_s_raw, wa_scales), (wb_s_raw, wb_scales)) for q in range(QUADS)]
+        for tile, src, q in scale_rows[:3]:
+            load_scale_rows(tile, 0, src, q)
         load_wab(0)
         load_wq(0)
-        for q in range(QUADS):
-            load_scale_rows(wa_s_raw, 0, wa_scales, q)
+        for tile, src, q in scale_rows[3:]:
+            load_scale_rows(tile, 0, src, q)
         nc.sync.dma_start(out=tab_w[:].bitcast(I32), in_=tab_words[0].rearrange("p t i -> p (t i)").bitcast(I32))
-        for q in range(QUADS):
-            load_scale_rows(wb_s_raw, 0, wb_scales, q)
         nc.gpsimd.dma_start(out=base_sb[:], in_=base.rearrange("(p s) -> p s", s=PACK))
+        nc.vector.tensor_copy(out=tab_s[0:16, :].bitcast(I32), in_=tab_s_raw[0:16, :].bitcast(I32))
+        nc.vector.tensor_copy(out=v_s_rows[:], in_=tab_s[:].indirect(offsets[:]))
+        for q in range(1, QUADS):
+            nc.sync.dma_start(out=v_s[32 * q : 32 * q + 4, :].bitcast(I32), in_=v_s_rows[4 * q : 4 * q + 4, :].bitcast(I32))
+        nc.vector.tensor_copy(out=v_s[0:4, :].bitcast(I32), in_=v_s_rows[0:4, :].bitcast(I32))
         deal_wab(0)
         load_wab(1)
         for t in range(PACK):
             round_wq(0, t)
-        for q in range(QUADS):
-            nc.vector.tensor_copy(out=tab_s[32 * q : 32 * q + 4, :].bitcast(I32), in_=tab_s_raw[32 * q : 32 * q + 4, :].bitcast(I32))
-        nc.vector.tensor_copy(out=v_s[:], in_=tab_s[:].indirect(offsets[:]))
-        deal_scales(wa_s, wa_s_raw, 0)
-        deal_scales(wa_s, wa_s_raw, 1)
-        deal_scales(wb_s, wb_s_raw, 0)
+        deal_scales(wa_s, wa_s_raw)
+        deal_scales(wb_s, wb_s_raw)
         load_wq(1)
         load_ws(0)
         quantize_w("wq", 0)
@@ -275,7 +277,7 @@ def tile_list_routed_credit_scorecard_kernel(
         beside = {
             0: [lambda: round_wq(1, 0), lambda: round_wq(1, 1)],
             1: [lambda: round_wq(1, 2), lambda: round_wq(1, 3)],
-            2: [lambda: deal_wab(1), lambda: deal_scales(wb_s, wb_s_raw, 1)],
+            2: [lambda: deal_wab(1)],
             3: [lambda: quantize_w("wq", 1), lambda: round_ws(0, 0), lambda: round_ws(0, 1)],
             4: [lambda: round_ws(0, 2), lambda: round_ws(0, 3)],
             5: [lambda: quantize_w("ws", 0), lambda: round_ws(1, 0), lambda: round_ws(1, 1)],
@@ -287,9 +289,9 @@ def tile_list_routed_credit_scorecard_kernel(
             11: [lambda: quantize_y(0, 256), lambda: round_y(256, 256, "scalar")],
             12: [lambda: score(512, 256, 0), lambda: score(512, 256, 2)],
             13: [lambda: quantize_y(256, 256), lambda: round_y(512, 256, "scalar")],
-            14: [],
+            14: [last_open],
             15: [lambda: quantize_y(512, 256)],
-            16: [lambda: score(768, 128, 0), last_open, lambda: round_y(768, 128, "scalar")],
+            16: [lambda: score(768, 128, 0), lambda: round_y(768, 128, "scalar")],
             17: [],
         }
 

@@ -23,7 +23,7 @@ RUN = 8
 BLOCKS = PASS // (RUN * PACK)
 CHUNK = 128
 QUADS = 4
-WB_ROW = 4
+GP_SHARE = 112
 
 
 def tile_list_routed_credit_scorecard_kernel(
@@ -177,11 +177,12 @@ def tile_list_routed_credit_scorecard_kernel(
                 op0=ALU.max if side == 0 else ALU.min, op1=ALU.mult,
             )
 
-        def join(group):
-            h_bf[group] = work.tile([P, group[2], 2, 2], BF16, name="h_bf", align_bytes=64)
-            nc.vector.tensor_tensor(
-                out=h_bf[group][:], in0=halves[group, 0][:].rearrange("p u n e -> p n u e"),
-                in1=halves[group, 1][:].rearrange("p u n e -> p n u e"), op=ALU.subtract,
+        def join(group, engine, n0, n1):
+            if n0 == 0:
+                h_bf[group] = stage.tile([P, group[2], 2, 2], BF16, name="h_bf", tag="h", align_bytes=64)
+            engine.tensor_tensor(
+                out=h_bf[group][:, n0:n1], in0=halves[group, 0][:].rearrange("p u n e -> p n u e")[:, n0:n1],
+                in1=halves[group, 1][:].rearrange("p u n e -> p n u e")[:, n0:n1], op=ALU.subtract,
             )
 
         def quantize_h(group):
@@ -214,7 +215,7 @@ def tile_list_routed_credit_scorecard_kernel(
                 nc.sync.dma_start(out=y_rows[:, :, js], in_=y_sb[j0][:])
 
         def round_y(j0, width, engine):
-            y_bf[j0] = work.tile([P, width * PACK], BF16, name="y_bf", align_bytes=64)
+            y_bf[j0] = ahead.tile([P, width * PACK], BF16, name="y_bf", align_bytes=64)
             dst = y_bf[j0][:].rearrange("p (c i s) -> p c s i", i=4, s=PACK)
             src = y_sb[j0][:].rearrange("p s (c i) -> p c s i", i=4)
             for c0 in range(0, width // 4, 32):
@@ -278,22 +279,26 @@ def tile_list_routed_credit_scorecard_kernel(
             0: [lambda: round_wq(1, 0), lambda: round_wq(1, 1)],
             1: [lambda: round_wq(1, 2), lambda: round_wq(1, 3)],
             2: [lambda: deal_wab(1)],
-            3: [lambda: quantize_w("wq", 1), lambda: round_ws(0, 0), lambda: round_ws(0, 1)],
+            3: [lambda: round_ws(0, 0), lambda: round_ws(0, 1)],
             4: [lambda: round_ws(0, 2), lambda: round_ws(0, 3)],
-            5: [lambda: quantize_w("ws", 0), lambda: round_ws(1, 0), lambda: round_ws(1, 1)],
+            5: [lambda: round_ws(1, 0), lambda: round_ws(1, 1)],
             6: [lambda: round_ws(1, 2), lambda: round_ws(1, 3)],
-            7: [lambda: quantize_w("ws", 1)],
-            8: [lambda: score(0, 256, 0), lambda: score(0, 256, 2)],
-            9: [lambda: round_y(0, 256, "scalar")],
-            10: [lambda: score(256, 256, 0), lambda: score(256, 256, 2)],
-            11: [lambda: quantize_y(0, 256), lambda: round_y(256, 256, "scalar")],
-            12: [lambda: score(512, 256, 0), lambda: score(512, 256, 2)],
-            13: [lambda: quantize_y(256, 256), lambda: round_y(512, 256, "scalar")],
-            14: [last_open],
-            15: [lambda: quantize_y(512, 256)],
+            7: [],
+            8: [],
+            9: [lambda: score(0, 256, 0), lambda: score(0, 256, 2)],
+            10: [lambda: round_y(0, 256, "scalar")],
+            11: [lambda: score(256, 256, 0), lambda: score(256, 256, 2)],
+            12: [lambda: round_y(256, 256, "scalar")],
+            13: [lambda: score(512, 256, 0), lambda: score(512, 256, 2)],
+            14: [lambda: round_y(512, 256, "scalar"), last_open],
+            15: [lambda: quantize_y(256, 256)],
             16: [lambda: score(768, 128, 0), lambda: round_y(768, 128, "scalar")],
-            17: [],
+            17: [lambda: quantize_y(512, 256)],
         }
+
+        with_h = {3: lambda: quantize_w("wq", 1), 5: lambda: quantize_w("ws", 0), 7: lambda: quantize_w("ws", 1),
+                  13: lambda: quantize_y(0, 256)}
+        shared = groups[:6]
 
         route_product(units[0])
         side_products(units[0])
@@ -304,16 +309,22 @@ def tile_list_routed_credit_scorecard_kernel(
                 route_product(units[u + 2])
             if u + 1 < len(units):
                 side_products(units[u + 1])
-            done = units[u - 1][0] if u > 0 and unit[1] == 0 else None
+            group, pair = unit
+            before = groups[groups.index(group) - 1] if u > 1 else None
+            done = before if before and pair == (1 if before in shared else 0) else None
             weigh(unit, 0)
             if done:
-                join(done)
+                join(done, nc.vector, GP_SHARE if done in shared else 0, done[2])
             weigh(unit, 1)
+            if u in with_h:
+                with_h[u]()
             if done:
                 quantize_h(done)
+            if pair == 1 and group in shared:
+                join(group, nc.gpsimd, 0, GP_SHARE)
             for step in beside[u]:
                 step()
-        join(groups[-1])
+        join(groups[-1], nc.vector, 0, groups[-1][2])
         quantize_h(groups[-1])
         quantize_y(768, 128)
 

from contextlib import ExitStack

import concourse.mybir as mybir

K, H, N, T, S = 512, 1024, 512, 4096, 1024
FLOPS = 2 * S * (3 * K * H + H * N)

F32 = mybir.dt.float32
BF16 = mybir.dt.bfloat16
I32 = mybir.dt.int32
U32 = mybir.dt.uint32
U16 = mybir.dt.uint16
U8 = mybir.dt.uint8
FP8X4 = mybir.dt.float8_e4m3fn_x4
FP4X4 = mybir.dt.float4_e2m1fn_x4
ALU = mybir.AluOpType
ACT = mybir.ActivationFunctionType

P = 128
PACK = 4
PASS = P * PACK
RUN = 8
BLOCKS = PASS // (RUN * PACK)
CHUNK = 128
QUADS = 4
GP_SHARE = 112


def tile_list_routed_credit_scorecard_kernel(
    tc, tab_words, tab_scales, offs, wq, wa_words, wa_scales, wb_words, wb_scales, ws, base, out_0, out_1, out_2
):
    nc = tc.nc
    with ExitStack() as ctx:
        keep = ctx.enter_context(tc.tile_pool(name="keep", bufs=1))
        stage = ctx.enter_context(tc.tile_pool(name="stage", bufs=1))
        work = ctx.enter_context(tc.tile_pool(name="work", bufs=2))
        ahead = ctx.enter_context(tc.tile_pool(name="ahead", bufs=4))
        psum = ctx.enter_context(tc.psum_pool(name="psum", bufs=2))

        offsets = keep.tile([P, S // 16], U16, name="offsets")
        tab_w = keep.tile([P, T], U32, name="tab_w", align_bytes=64)
        tab_s = stage.tile([P, T], U8, name="tab_s", tag="c", align_bytes=64)
        tab_s_raw = keep.tile([P, T], U8, name="tab_s_raw", align_bytes=64)
        v_w = keep.tile([P, S], U32, name="v_w", align_bytes=64)
        v_s_rows = keep.tile([P, S], U8, name="v_s_rows", align_bytes=64)
        v_s = keep.tile([P, S], U8, name="v_s", align_bytes=64)
        wa_s_raw = keep.tile([P, H], U8, name="wa_s_raw", align_bytes=64)
        wb_s_raw = keep.tile([P, H], U8, name="wb_s_raw", align_bytes=64)
        wa_s = keep.tile([P, H], U8, name="wa_s", align_bytes=64)
        wb_s = keep.tile([P, H], U8, name="wb_s", align_bytes=64)
        base_sb = keep.tile([P, PACK], F32, name="base_sb")
        wq_w = [keep.tile([P, PASS], U32, name="wq_w%d" % b, align_bytes=64) for b in range(2)]
        wq_s = [keep.tile([P, PASS], U8, name="wq_s%d" % b, align_bytes=64) for b in range(2)]
        wa_w = {}
        wb_w = {}
        ws_w = [keep.tile([P, N], U32, name="ws_w%d" % b, align_bytes=64) for b in range(2)]
        ws_s = [keep.tile([P, N], U8, name="ws_s%d" % b, align_bytes=64) for b in range(2)]
        h_w = [keep.tile([P, S], U32, name="h_w%d" % b, align_bytes=64) for b in range(2)]
        h_s = [keep.tile([P, S], U8, name="h_s%d" % b, align_bytes=64) for b in range(2)]
        y_w = keep.tile([P, S], U32, name="y_w", align_bytes=64)
        y_s = keep.tile([P, S], U8, name="y_s", align_bytes=64)

        wq_rows = wq.rearrange("(p j) r -> p j r", j=PACK)
        wa_src = wa_words[0].bitcast(I32)
        wb_src = wb_words[0].rearrange("p c i -> p (c i)").bitcast(I32)
        y_rows = out_0.rearrange("(p s) j -> p s j", s=PACK)
        y_w_dst = out_1[0].rearrange("p m t -> p (m t)").bitcast(I32)

        raw = {}
        rounded = {}

        def load_wq(b):
            raw["wq", b] = stage.tile([P, PACK, PASS], F32, name="wq_raw", tag="ac"[b], align_bytes=64)
            nc.sync.dma_start(out=raw["wq", b][:], in_=wq_rows[:, :, PASS * b : PASS * (b + 1)])

        def load_wab(b):
            both = stage.tile([P, PASS // 2 + PASS], I32, name="wab_raw", tag="d", align_bytes=64)
            raw["wa", b] = both[:, 0 : PASS // 2]
            raw["wb", b] = both[:, PASS // 2 : PASS // 2 + PASS]
            nc.sync.dma_start(out=raw["wa", b], in_=wa_src[:, PASS // 2 * b : PASS // 2 * (b + 1)])
            nc.sync.dma_start(out=raw["wb", b], in_=wb_src[:, PASS * b : PASS * (b + 1)])

        def load_ws(b):
            raw["ws", b] = stage.tile([P, PACK, N], F32, name="ws_raw", tag="ab"[b], align_bytes=64)
            rows = ws[PASS * b : PASS * (b + 1), :].rearrange("(q t i) n -> t q i n", t=PACK, i=RUN)
            for t in range(PACK):
                nc.sync.dma_start(out=raw["ws", b][:, t, :], in_=rows[t])

        def deal_wab(b):
            both = stage.tile([P, PASS // 2 + PASS], U32, name="wab_w", tag=("w", "g")[b], align_bytes=64)
            wa_w[b] = both[:, 0 : PASS // 2]
            wb_w[b] = both[:, PASS // 2 : PASS // 2 + PASS]
            nc.scalar.copy(
                out=wa_w[b].rearrange("p (t q i) -> p t q i", t=PACK, q=BLOCKS),
                in_=raw["wa", b].bitcast(U32).rearrange("p (q t i) -> p t q i", t=PACK, q=BLOCKS),
            )
            nc.scalar.copy(
                out=wb_w[b].rearrange("p (t q i) -> p t q i", t=PACK, q=BLOCKS),
                in_=raw["wb", b].bitcast(U32).rearrange("p (q t i) -> p t q i", t=PACK, q=BLOCKS),
            )

        def deal_scales(dst, src):
            for q in range(QUADS):
                rows = slice(32 * q, 32 * q + 4)
                nc.scalar.copy(
                    out=dst[rows, :].bitcast(U32).rearrange("p (b t q i) -> p b t q i", b=2, t=PACK, q=BLOCKS),
                    in_=src[rows, :].bitcast(U32).rearrange("p (b q t i) -> p b t q i", b=2, t=PACK, q=BLOCKS),
                )

        def round_wq(b, t):
            if t == 0 and b == 0:
                rounded["wq", b] = stage.tile([P, PASS * PACK], BF16, name="w_bf", tag="b", align_bytes=64)
            elif t == 0:
                rounded["wq", b] = stage.tile([P, PASS * PACK], BF16, name="w_bf", tag="e", align_bytes=64)
            dst = rounded["wq", b][:].rearrange("p (t q h i j) -> p t h q j i", t=PACK, q=BLOCKS, h=2, j=PACK)
            src = raw["wq", b][:].rearrange("p j (q t h i) -> p t h q j i", t=PACK, h=2, i=RUN // 2)
            for h in range(2):
                nc.scalar.activation(out=dst[:, t, h], in_=src[:, t, h], func=ACT.Identity)

        def round_ws(b, part):
            if part == 0:
                rounded["ws", b] = stage.tile([P, N * PACK], BF16, name="w_bf", tag="fe"[b], align_bytes=64)
            ms = slice(64 * (part // 2), 64 * (part // 2 + 1))
            dst = rounded["ws", b][:].rearrange("p (u e m t) -> p u m t e", u=2, e=2, t=PACK)
            src = raw["ws", b][:].rearrange("p t (m u e) -> p u m t e", u=2, e=2)
            nc.scalar.activation(out=dst[:, part % 2, ms], in_=src[:, part % 2, ms], func=ACT.Identity)

        def quantize_w(kind, b):
            words, scales = (wq_w, wq_s) if kind == "wq" else (ws_w, ws_s)
            nc.vector.quantize_mx(out=words[b][:].bitcast(FP8X4), scales=scales[b][:], in_=rounded[kind, b][:])

        def gather_words(j0, j1):
            nc.vector.tensor_copy(out=v_w[:, j0:j1], in_=tab_w[:].indirect(offsets[:, j0 // 16 : j1 // 16]))

        banks = {}
        halves = {}
        h_bf = {}

        def product(name, unit, stationary):
            (b, j0, width), pair = unit
            js = slice(j0, j0 + width)
            bank = psum.tile([P, 2, width], F32, name=name)
            for e in range(2):
                words, scales = stationary(b, 2 * pair + e)
                nc.tensor.matmul_mx(out=bank[:, e, :], lhsT=words, lhsT_scale=scales, rhs=v_w[:, js].bitcast(FP8X4),
                                    rhs_scale=v_s[:, js], start=True, stop=True)
            return bank[:].rearrange("p e n -> p n e")

        def wq_slot(b, t):
            cols = slice(P * t, P * (t + 1))
            return wq_w[b][:, cols].bitcast(FP8X4), wq_s[b][:, cols]

        def wa_slot(b, t):
            return wa_w[b][:, P // 2 * t : P // 2 * (t + 1)].bitcast(FP4X4), wa_s[:, PASS * b + P * t : PASS * b + P * (t + 1)]

        def wb_slot(b, t):
            return wb_w[b][:, P * t : P * (t + 1)].bitcast(FP8X4), wb_s[:, PASS * b + P * t : PASS * b + P * (t + 1)]

        def route_product(unit):
            route = product("route", unit, wq_slot)
            if unit in units[:3]:
                banks[unit, "route"] = stage.tile([P, unit[0][2], 2], F32, name="route_sb", tag="egf"[units.index(unit)], align_bytes=64)
            else:
                banks[unit, "route"] = ahead.tile([P, unit[0][2], 2], F32, name="route_sb")
            nc.scalar.copy(out=banks[unit, "route"][:], in_=route)

        def side_products(unit):
            banks[unit, 0] = product("left", unit, wa_slot)
            banks[unit, 1] = product("right", unit, wb_slot)

        def weigh(unit, side):
            group, pair = unit
            if pair == 0:
                halves[group, side] = work.tile([P, 2, group[2], 2], BF16, name="half%d" % side, align_bytes=64)
            nc.vector.scalar_tensor_tensor(
                out=halves[group, side][:, pair], in0=banks[unit, "route"][:], scalar=0.0, in1=banks[unit, side],
                op0=ALU.max if side == 0 else ALU.min, op1=ALU.mult,
            )

        def join(group, engine, n0, n1):
            if n0 == 0:
                h_bf[group] = stage.tile([P, group[2], 2, 2], BF16, name="h_bf", tag="h", align_bytes=64)
            engine.tensor_tensor(
                out=h_bf[group][:, n0:n1], in0=halves[group, 0][:].rearrange("p u n e -> p n u e")[:, n0:n1],
                in1=halves[group, 1][:].rearrange("p u n e -> p n u e")[:, n0:n1], op=ALU.subtract,
            )

        def quantize_h(group):
            b, j0, width = group
            js = slice(j0, j0 + width)
            nc.vector.quantize_mx(out=h_w[b][:, js].bitcast(FP8X4), scales=h_s[b][:, js],
                                  in_=h_bf[group][:].rearrange("p n u e -> p (n u e)"))

        y_sb = {}
        y_bf = {}

        def score_pass(bank, s, b, js, start, stop):
            cols = slice(P * s, P * (s + 1))
            nc.tensor.matmul_mx(out=bank, lhsT=ws_w[b][:, cols].bitcast(FP8X4), lhsT_scale=ws_s[b][:, cols],
                                rhs=h_w[b][:, js].bitcast(FP8X4), rhs_scale=h_s[b][:, js], start=start, stop=stop)

        def score(j0, width, s0):
            js = slice(j0, j0 + width)
            if s0 == 0:
                y_sb[j0] = work.tile([P, PACK, width], F32, name="y_sb")
            per_bank = 512 // width
            bank = psum.tile([P, per_bank, width], F32, name="score")
            for s in range(s0, s0 + per_bank):
                for b in range(2):
                    score_pass(bank[:, s - s0, :], s, b, js, b == 0, b == 1)
            for s in range(s0, s0 + per_bank):
                nc.scalar.activation(out=y_sb[j0][:, s, :], in_=bank[:, s - s0, :], func=ACT.Identity,
                                     bias=base_sb[:, s : s + 1])
            if s0 + per_bank == PACK:
                nc.sync.dma_start(out=y_rows[:, :, js], in_=y_sb[j0][:])

        def round_y(j0, width, engine):
            y_bf[j0] = ahead.tile([P, width * PACK], BF16, name="y_bf", align_bytes=64)
            dst = y_bf[j0][:].rearrange("p (c i s) -> p c s i", i=4, s=PACK)
            src = y_sb[j0][:].rearrange("p s (c i) -> p c s i", i=4)
            for c0 in range(0, width // 4, 32):
                if engine == "scalar":
                    nc.scalar.copy(out=dst[:, c0 : c0 + 32], in_=src[:, c0 : c0 + 32])
                else:
                    nc.vector.tensor_copy(out=dst[:, c0 : c0 + 32], in_=src[:, c0 : c0 + 32])

        def quantize_y(j0, width):
            js = slice(j0, j0 + width)
            nc.vector.quantize_mx(out=y_w[:, js].bitcast(FP8X4), scales=y_s[:, js], in_=y_bf[j0][:])
            nc.sync.dma_start(out=y_w_dst[:, js], in_=y_w[:, js].bitcast(I32))

        def load_scale_rows(tile, row0, src, q):
            nc.sync.dma_start(out=tile[32 * q + row0 : 32 * q + row0 + 4, :].bitcast(I32), in_=src[0, 4 * q : 4 * q + 4, :].bitcast(I32))

        nc.vector.memset(tab_s[:].bitcast(I32), 0)
        nc.vector.memset(v_s[:].bitcast(I32), 0)
        nc.vector.memset(wa_s[:].bitcast(I32), 0)
        nc.vector.memset(wb_s[:].bitcast(I32), 0)
        nc.sync.dma_start(offsets[:], offs)
        nc.sync.dma_start(out=tab_s_raw[0:16, :].bitcast(I32), in_=tab_scales[0].bitcast(I32))
        scale_rows = [(tile, src, q) for tile, src in ((wa_s_raw, wa_scales), (wb_s_raw, wb_scales)) for q in range(QUADS)]
        for tile, src, q in scale_rows[:3]:
            load_scale_rows(tile, 0, src, q)
        load_wab(0)
        load_wq(0)
        for tile, src, q in scale_rows[3:]:
            load_scale_rows(tile, 0, src, q)
        nc.sync.dma_start(out=tab_w[:].bitcast(I32), in_=tab_words[0].rearrange("p t i -> p (t i)").bitcast(I32))
        nc.gpsimd.dma_start(out=base_sb[:], in_=base.rearrange("(p s) -> p s", s=PACK))
        nc.vector.tensor_copy(out=tab_s[0:16, :].bitcast(I32), in_=tab_s_raw[0:16, :].bitcast(I32))
        nc.vector.tensor_copy(out=v_s_rows[:], in_=tab_s[:].indirect(offsets[:]))
        for q in range(1, QUADS):
            nc.sync.dma_start(out=v_s[32 * q : 32 * q + 4, :].bitcast(I32), in_=v_s_rows[4 * q : 4 * q + 4, :].bitcast(I32))
        nc.vector.tensor_copy(out=v_s[0:4, :].bitcast(I32), in_=v_s_rows[0:4, :].bitcast(I32))
        deal_wab(0)
        load_wab(1)
        for t in range(PACK):
            round_wq(0, t)
        deal_scales(wa_s, wa_s_raw)
        deal_scales(wb_s, wb_s_raw)
        load_wq(1)
        load_ws(0)
        quantize_w("wq", 0)
        load_ws(1)
        gather_words(0, 256)
        gather_words(256, 512)

        groups = [(0, 0, 256), (0, 256, 256), (0, 512, 256), (1, 0, 256), (1, 256, 256), (1, 512, 256),
                  (0, 768, 256), (1, 768, 128), (1, 896, 128)]
        units = [(group, pair) for group in groups for pair in range(2)]

        def last_open():
            js = slice(S - CHUNK, S)
            banks["last"] = psum.tile([P, PACK, CHUNK], F32, name="score")
            for s in range(PACK):
                score_pass(banks["last"][:, s, :], s, 0, js, s == 0, False)

        beside = {
            0: [lambda: round_wq(1, 0), lambda: round_wq(1, 1)],
            1: [lambda: round_wq(1, 2), lambda: round_wq(1, 3)],
            2: [lambda: deal_wab(1)],
            3: [lambda: round_ws(0, 0), lambda: round_ws(0, 1)],
            4: [lambda: round_ws(0, 2), lambda: round_ws(0, 3)],
            5: [lambda: round_ws(1, 0), lambda: round_ws(1, 1)],
            6: [lambda: round_ws(1, 2), lambda: round_ws(1, 3)],
            7: [],
            8: [],
            9: [lambda: score(0, 256, 0), lambda: score(0, 256, 2)],
            10: [lambda: round_y(0, 256, "scalar")],
            11: [lambda: score(256, 256, 0), lambda: score(256, 256, 2)],
            12: [lambda: round_y(256, 256, "scalar")],
            13: [lambda: score(512, 256, 0), lambda: score(512, 256, 2)],
            14: [lambda: round_y(512, 256, "scalar"), last_open],
            15: [lambda: quantize_y(256, 256)],
            16: [lambda: score(768, 128, 0), lambda: round_y(768, 128, "scalar")],
            17: [lambda: quantize_y(512, 256)],
        }

        with_h = {3: lambda: quantize_w("wq", 1), 5: lambda: quantize_w("ws", 0), 7: lambda: quantize_w("ws", 1),
                  13: lambda: quantize_y(0, 256)}
        shared = groups[:6]

        route_product(units[0])
        side_products(units[0])
        route_product(units[1])
        gather_words(512, 1024)
        for u, unit in enumerate(units):
            if u + 2 < len(units):
                route_product(units[u + 2])
            if u + 1 < len(units):
                side_products(units[u + 1])
            group, pair = unit
            before = groups[groups.index(group) - 1] if u > 1 else None
            done = before if before and pair == (1 if before in shared else 0) else None
            weigh(unit, 0)
            if done:
                join(done, nc.vector, GP_SHARE if done in shared else 0, done[2])
            weigh(unit, 1)
            if u in with_h:
                with_h[u]()
            if done:
                quantize_h(done)
            if pair == 1 and group in shared:
                join(group, nc.gpsimd, 0, GP_SHARE)
            for step in beside[u]:
                step()
        join(groups[-1], nc.vector, 0, groups[-1][2])
        quantize_h(groups[-1])
        quantize_y(768, 128)

        j0 = S - CHUNK
        js = slice(j0, S)
        bank = banks["last"]
        for s in range(PACK):
            score_pass(bank[:, s, :], s, 1, js, False, s == PACK - 1)
        y_last = work.tile([P, PACK, CHUNK], F32, name="y_sb")
        y_last_bf = work.tile([P, CHUNK * PACK], BF16, name="y_bf", align_bytes=64)
        for half in range(2):
            ns = slice(CHUNK // 2 * half, CHUNK // 2 * (half + 1))
            nc.vector.tensor_tensor(out=y_last[:, :, ns], in0=bank[:, :, ns],
                                    in1=base_sb[:].unsqueeze(2).to_broadcast([P, PACK, CHUNK // 2]), op=ALU.add)
        nc.sync.dma_start(out=y_rows[:, :, js], in_=y_last[:])
        for half in range(2):
            es = slice(CHUNK * 2 * half, CHUNK * 2 * (half + 1))
            ns = slice(CHUNK // 2 * half, CHUNK // 2 * (half + 1))
            nc.vector.tensor_copy(out=y_last_bf[:, es].rearrange("p (c i s) -> p c s i", i=4, s=PACK),
                                  in_=y_last[:, :, ns].rearrange("p s (c i) -> p c s i", i=4))
        for half in range(2):
            es = slice(CHUNK * 2 * half, CHUNK * 2 * (half + 1))
            ns = slice(j0 + CHUNK // 2 * half, j0 + CHUNK // 2 * (half + 1))
            nc.vector.quantize_mx(out=y_w[:, ns].bitcast(FP8X4), scales=y_s[:, ns], in_=y_last_bf[:, es])
        nc.sync.dma_start(out=y_w_dst[:, js], in_=y_w[:, js].bitcast(I32))
        for q in range(QUADS):
            engine = nc.scalar if q % 2 else nc.sync
            engine.dma_start(out=out_2[0, 4 * q : 4 * q + 4, :].bitcast(I32), in_=y_s[32 * q : 32 * q + 4, :].bitcast(I32))
